import numpy as np
import ml_dtypes


def mxq(x, axis, fmt="e4m3"):
    dtype, down = {"e4m3": (ml_dtypes.float8_e4m3fn, 7), "e5m2": (ml_dtypes.float8_e5m2, 14)}[fmt]
    v = np.moveaxis(np.asarray(x, np.float32).astype(ml_dtypes.bfloat16).astype(np.float64), axis, -1)
    blocks = v.reshape(v.shape[:-1] + (-1, 32))
    amax = np.abs(blocks).max(-1, keepdims=True)
    byte = np.maximum(np.where(amax > 0, np.frexp(amax)[1] - 1 + 127, 0) - down, 1)
    scale = np.exp2(byte - 127.0)
    codes = (blocks / scale).astype(np.float32).astype(dtype).astype(np.float64)
    return np.moveaxis((codes * scale).reshape(v.shape), -1, axis)


WIDE = False


def mx_kscale(k):
    if not WIDE:
        return np.ones(k)
    levels = np.array([30, -30])
    if k % 512:
        return np.exp2(np.random.permutation(np.resize(levels, k // 32))).repeat(32)
    a = np.empty((k // 512, 16))
    for p in range(k // 512):
        a[p, :8] = np.random.permutation(np.resize(levels, 8))
        for g in range(8):
            far = levels[np.abs(levels - a[p, g]) >= 10]
            a[p, g + 8] = far[np.random.randint(len(far))]
    return np.exp2(a.ravel()).repeat(32)


def f64(x):
    return np.asarray(x).astype(np.float64)


def striped(idx):
    return np.tile(np.asarray(idx).reshape(-1, 16).T, (8, 1)).astype(np.uint16)


def unstriped(offs):
    return offs[:16].T.reshape(-1).astype(np.int64)


E2M1 = np.array([0.0, 0.5, 1.0, 1.5, 2.0, 3.0, 4.0, 6.0, -0.0, -0.5, -1.0, -1.5, -2.0, -3.0, -4.0, -6.0])


def pack_weight(w, fmt):
    k, n = w.shape
    w = f64(np.asarray(w, np.float32).astype(ml_dtypes.bfloat16)).reshape(k // 32, 32, n)
    amax = np.abs(w).max(1)
    if fmt == "e4m3":
        byte = np.frexp(amax)[1] - 1 + 127 - 7
    else:
        mant, ex = np.frexp(amax / 6.0)
        byte = np.where(mant > 0.5, ex, ex - 1) + 127
    byte = np.clip(np.where(amax > 0, byte, 1), 1, 254)
    scaled = (w * np.exp2(127.0 - byte)[:, None, :]).reshape(k, n).astype(np.float32)
    by_word = np.ascontiguousarray(scaled.reshape(k // 512, 128, 4, n).transpose(0, 1, 3, 2))
    if fmt == "e4m3":
        words = by_word.astype(ml_dtypes.float8_e4m3fn).view(np.uint8)
    else:
        c = by_word.astype(ml_dtypes.float4_e2m1fn).view(np.uint8) & 0xF
        words = (c[..., 0::2] | (c[..., 1::2] << 4)).reshape(k // 512, 128, 2 * n)
    return np.ascontiguousarray(words), np.ascontiguousarray(byte.astype(np.uint8).reshape(k // 512, 16, n))


def unpack_weight(words, scales, fmt):
    g, _, n = scales.shape
    words = np.ascontiguousarray(words).reshape(g, 128, n, -1)
    if fmt == "e4m3":
        vals = words.view(ml_dtypes.float8_e4m3fn).astype(np.float64)
    else:
        nib = np.empty((g, 128, n, 4), np.uint8)
        nib[..., 0::2] = words & 0xF
        nib[..., 1::2] = words >> 4
        vals = E2M1[nib]
    vals = vals * np.repeat(np.exp2(scales.astype(np.float64) - 127.0), 8, axis=1)[..., None]
    return vals.transpose(0, 1, 3, 2).reshape(g * 512, n)


K, N, T, J = 512, 512, 1024, 512


def setup_inputs():
    n = np.random.standard_normal
    idx = np.random.permutation(T)[:J]
    fk = mx_kscale(K)
    fn = mx_kscale(N)
    xtp = pack_weight(n((K, T)) / fk[:, None], "e4m3")
    wnp = pack_weight(n((K, N)) * 1 / np.sqrt(K) * fk[:, None], "e2m1")
    wtp = pack_weight(n((N, K)) * 1 / np.sqrt(N) / fn[:, None], "e4m3")
    return {
        "xt_words": xtp[0],
        "xt_scales": xtp[1],
        "wn_words": wnp[0],
        "wn_scales": wnp[1],
        "te": (n((N, T))).astype(np.float32),
        "us": (np.random.uniform(0.5, 2.0, (N, 1)) * fn[:, None]).astype(np.float32),
        "wt_words": wtp[0],
        "wt_scales": wtp[1],
        "run": (0.3 * n((K, T))).astype(np.float32),
        "offs": striped(idx),
    }


def reference(xt_words, xt_scales, wn_words, wn_scales, te, us, wt_words, wt_scales, run, offs):
    idx = unstriped(offs)
    xtu = unpack_weight(xt_words, xt_scales, "e4m3")
    wnu = unpack_weight(wn_words, wn_scales, "e2m1")
    wtu = unpack_weight(wt_words, wt_scales, "e4m3")
    xtidxg = xtu[:, idx]
    p = wnu.T @ xtidxg
    d = (p - f64(te)[:, idx]) * f64(us)
    dq = mxq(d, 0, "e5m2")
    q = wtu.T @ dq
    qp = np.zeros((K, T))
    qp[:, idx] = q
    y = qp + f64(run)
    return y

@@ -1,0 +1,202 @@
+from contextlib import ExitStack
+
+import concourse.mybir as mybir
+from concourse.masks import make_identity
+
+K, N, T, J = 512, 512, 1024, 512
+FLOPS = 2 * K * N * J * 2
+
+F32 = mybir.dt.float32
+BF16 = mybir.dt.bfloat16
+I32 = mybir.dt.int32
+U32 = mybir.dt.uint32
+U16 = mybir.dt.uint16
+U8 = mybir.dt.uint8
+E4M3X4 = mybir.dt.float8_e4m3fn_x4
+E5M2X4 = mybir.dt.float8_e5m2_x4
+E2M1X4 = mybir.dt.float4_e2m1fn_x4
+COPY = mybir.ActivationFunctionType.Copy
+SUB = mybir.AluOpType.subtract
+ADD = mybir.AluOpType.add
+
+P = 128
+PACK = 4
+HALF = J // 2
+LANES = 16
+BANK = 512
+
+
+def load_scale_rows(queue, plane, scales):
+    for i in range(4):
+        queue.dma_start(plane[i:P:32, :].bitcast(I32), scales[0, i:16:4, :].bitcast(I32))
+
+
+def tile_moe_expert_taught_by_page_kernel(
+    tc, xt_words, xt_scales, wn_words, wn_scales, te, us, wt_words, wt_scales, run, offs, out
+):
+    nc = tc.nc
+    with ExitStack() as ctx:
+        keep = ctx.enter_context(tc.tile_pool(name="keep", bufs=1))
+        psum = ctx.enter_context(tc.psum_pool(name="psum", bufs=1))
+
+        offsets = keep.tile([P, J // LANES], U16, name="offsets")
+        wn_plane = keep.tile([P, N], U8, name="wn_plane", align_bytes=64)
+        xt_plane = keep.tile([P, T], U8, name="xt_plane", align_bytes=64)
+        wt_plane = keep.tile([P, K], U8, name="wt_plane", align_bytes=64)
+        d_codes = keep.tile([P, J], I32, name="d_codes", align_bytes=64)
+        d_plane = keep.tile([P, J], U8, name="d_plane", align_bytes=64)
+        xt_tile = keep.tile([P, T], I32, name="xt_tile", align_bytes=64)
+        wn_tile = keep.tile([P, 2 * N], U8, name="wn_tile", align_bytes=64)
+        wt_tile = keep.tile([P, K], I32, name="wt_tile", align_bytes=64)
+        te_tiles = [keep.tile([P, T], F32, name="te%d" % r) for r in range(PACK)]
+        run_tiles = [keep.tile([P, T], F32, name="run%d" % c) for c in range(4)]
+        windows = [keep.tile([P, T], F32, name="window%d" % w) for w in range(3)]
+        us_tile = keep.tile([P, PACK], F32, name="us_tile")
+        neg_us = keep.tile([P, PACK], F32, name="neg_us")
+        ident = keep.tile([P, P], F32, name="ident")
+
+        for plane in (wn_plane, xt_plane, wt_plane):
+            nc.vector.memset(plane[:].bitcast(I32), 0)
+
+        nc.sync.dma_start(offsets[:], offs)
+        load_scale_rows(nc.sync, wn_plane, wn_scales)
+        nc.sync.dma_start(xt_tile[:], xt_words[0].rearrange("p t r -> p (t r)").bitcast(I32))
+        nc.sync.dma_start(wn_tile[:].bitcast(I32), wn_words[0].bitcast(I32))
+        te_rows = te.rearrange("(p r) t -> p r t", r=PACK)
+        nc.sync.dma_start(te_tiles[0][:], te_rows[:, 0, :])
+        load_scale_rows(nc.sync, xt_plane, xt_scales)
+        for r in range(1, PACK):
+            nc.sync.dma_start(te_tiles[r][:], te_rows[:, r, :])
+        nc.gpsimd.dma_start(us_tile[:], us.rearrange("(p r) o -> p (r o)", r=PACK))
+        nc.sync.dma_start(wt_tile[:], wt_words[0].rearrange("p k r -> p (k r)").bitcast(I32))
+        load_scale_rows(nc.sync, wt_plane, wt_scales)
+        for c in range(4):
+            nc.sync.dma_start(run_tiles[c][:], run[c * P : (c + 1) * P, :])
+
+        make_identity(nc, ident[:])
+        nc.vector.memset(d_codes[:, HALF:J], 0)
+        nc.vector.memset(d_plane[:, HALF:J].bitcast(I32), 0)
+        for window in windows:
+            nc.vector.memset(window[:], 0.0)
+        nc.scalar.mul(neg_us[:], us_tile[:], -1.0)
+
+        wn_perm = keep.tile([P, 2 * N], U8, name="wn_perm", align_bytes=64)
+        wn_plane_perm = keep.tile([P, N], U8, name="wn_plane_perm", align_bytes=64)
+        nc.vector.tensor_copy(
+            wn_plane_perm[:].rearrange("p (r m) -> p r m", r=PACK),
+            wn_plane[:].rearrange("p (m r) -> p r m", r=PACK),
+        )
+        nc.vector.tensor_copy(
+            wn_perm[:].bitcast(U16).rearrange("p (r m) -> p r m", r=PACK),
+            wn_tile[:].bitcast(U16).rearrange("p (m r) -> p r m", r=PACK),
+        )
+
+        def listed(h):
+            return offsets[:, h * HALF // LANES : (h + 1) * HALF // LANES]
+
+        xg_words = [keep.tile([P, HALF], U32, name="xg_words%d" % h, align_bytes=64) for h in range(2)]
+        xg_plane = [keep.tile([P, HALF], U8, name="xg_plane%d" % h, align_bytes=64) for h in range(2)]
+        for h in range(2):
+            nc.vector.tensor_copy(xg_words[h][:], xt_tile[:].bitcast(U32).indirect(listed(h)))
+        for h in range(2):
+            nc.vector.tensor_copy(xg_plane[h][:], xt_plane[:].indirect(listed(h)))
+
+        p_tiles = {}
+        for h in range(2):
+            for r in range(PACK):
+                acc = psum.tile([P, HALF], F32, name="p_acc", tag="mx", bufs=4)
+                nc.tensor.matmul_mx(
+                    acc[:],
+                    lhsT=wn_perm[:, 2 * P * r : 2 * P * (r + 1)].bitcast(E2M1X4),
+                    lhsT_scale=wn_plane_perm[:, P * r : P * (r + 1)],
+                    rhs=xg_words[h][:].bitcast(E4M3X4),
+                    rhs_scale=xg_plane[h][:],
+                    start=True,
+                    stop=True,
+                )
+                p_tiles[h, r] = keep.tile([P, HALF], F32, name="p%d_%d" % (h, r))
+                nc.scalar.copy(p_tiles[h, r][:], acc[:])
+
+        def difference(h, r, pairs, tag):
+            diff = keep.tile([P, HALF], F32, name="diff%d_%d" % (h, r), tag=tag, align_bytes=64)
+            nc.vector.tensor_tensor(diff[:], te_tiles[r][:].indirect(listed(h)), p_tiles[h, r][:], SUB)
+            nc.scalar.activation(pairs[:, r // 2, :, r % 2], diff[:], COPY, scale=neg_us[:, r : r + 1])
+
+        def weave(h, pairs, tag):
+            d_half = keep.tile([P, HALF * PACK], BF16, name="d_half%d" % h, tag=tag, align_bytes=64)
+            nc.scalar.copy(
+                d_half[:].bitcast(F32).rearrange("p (j u) -> p j u", u=2),
+                pairs[:].rearrange("p u j e -> p u (j e)").bitcast(F32).rearrange("p u j -> p j u"),
+            )
+            return d_half
+
+        def quantise(h, d_half):
+            cols = slice(h * HALF, (h + 1) * HALF)
+            nc.vector.quantize_mx(d_codes[:, cols].bitcast(E5M2X4), d_plane[:, cols], d_half[:])
+
+        def way_back(c):
+            acc = psum.tile([P, J], F32, name="q_acc", tag="mx", bufs=4)
+            nc.tensor.matmul_mx(
+                acc[:],
+                lhsT=wt_tile[:, P * c : P * (c + 1)].bitcast(E4M3X4),
+                lhsT_scale=wt_plane[:, P * c : P * (c + 1)],
+                rhs=d_codes[:].bitcast(E5M2X4),
+                rhs_scale=d_plane[:],
+                start=True,
+                stop=True,
+            )
+            return acc
+
+        def scatter(acc, window, lo, hi, tag):
+            q_part = keep.tile([P, hi - lo], F32, name="q_" + tag, tag=tag, align_bytes=64)
+            nc.scalar.copy(q_part[:], acc[:, lo:hi])
+            nc.vector.tensor_copy(window[:].indirect(offsets[:, lo // LANES : hi // LANES]), q_part[:])
+
+        def add_on_tensor_engine(c, window):
+            turned = keep.tile([P, T], F32, name="turned", tag="turned", bufs=2)
+            result = keep.tile([P, T], F32, name="result", tag="result", bufs=3)
+            for b in range(T // BANK):
+                bank = psum.tile([P, BANK], F32, name="sum_bank", tag="sum_bank", bufs=2)
+                for s in range(BANK // P):
+                    cols = slice(b * BANK + s * P, b * BANK + (s + 1) * P)
+                    here = slice(s * P, (s + 1) * P)
+                    nc.tensor.matmul(bank[:, here], run_tiles[c][:, cols], ident[:], start=True, stop=False, is_transpose=True)
+                    nc.tensor.matmul(bank[:, here], window[:, cols], ident[:], start=False, stop=True, is_transpose=True)
+                nc.scalar.copy(turned[:, b * BANK : (b + 1) * BANK], bank[:])
+            for b in range(T // BANK):
+                bank = psum.tile([P, BANK], F32, name="back_bank", tag="back_bank", bufs=2)
+                for s in range(BANK // P):
+                    cols = slice(b * BANK + s * P, b * BANK + (s + 1) * P)
+                    nc.tensor.transpose(bank[:, s * P : (s + 1) * P], turned[:, cols], ident[:])
+                cols = slice(b * BANK, (b + 1) * BANK)
+                nc.scalar.copy(result[:, cols], bank[:])
+                nc.scalar.dma_start(out[c * P : (c + 1) * P, cols], result[:, cols])
+
+        pairs0 = keep.tile([P, 2, HALF, 2], BF16, name="pairs0", align_bytes=64)
+        pairs1 = keep.tile([P, 2, HALF, 2], BF16, name="pairs1", tag="after_weave1", align_bytes=64)
+        for r in range(PACK):
+            difference(0, r, pairs0, "diff0_%d" % r)
+        d_first = weave(0, pairs0, "after_quantise0")
+        difference(1, 0, pairs1, "diff1_0")
+        difference(1, 1, pairs1, "diff1_1")
+        quantise(0, d_first)
+        early = [way_back(c) for c in range(2)]
+        difference(1, 2, pairs1, "after_quantise0")
+        difference(1, 3, pairs1, "diff1_3")
+        scatter(early[0], windows[0], 0, HALF, "early0")
+        d_second = weave(1, pairs1, "d_second")
+        quantise(1, d_second)
+        scatter(early[1], windows[1], 0, HALF, "after_weave1")
+        late = [way_back(c) for c in range(4)]
+        scatter(late[0], windows[0], HALF, J, "late0")
+        scatter(late[1], windows[1], HALF, J, "late1")
+        scatter(late[2], windows[2], 0, J, "late2")
+        add_on_tensor_engine(0, windows[0])
+        scatter(late[3], windows[0], 0, J, "late3")
+        add_on_tensor_engine(1, windows[1])
+        add_on_tensor_engine(2, windows[2])
+        last = keep.tile([P, T], F32, name="last")
+        for b in range(T // BANK):
+            cols = slice(b * BANK, (b + 1) * BANK)
+            nc.vector.tensor_tensor(last[:, cols], windows[0][:, cols], run_tiles[3][:, cols], ADD)
+            nc.sync.dma_start(out[3 * P : 4 * P, cols], last[:, cols])

@@ -1,7 +1,6 @@
 from contextlib import ExitStack
 
 import concourse.mybir as mybir
-from concourse.masks import make_identity
 
 K, N, T, J = 512, 512, 1024, 512
 FLOPS = 2 * K * N * J * 2
@@ -53,7 +52,6 @@ def tile_moe_expert_taught_by_page_kernel(
         windows = [keep.tile([P, T], F32, name="window%d" % w) for w in range(3)]
         us_tile = keep.tile([P, PACK], F32, name="us_tile")
         neg_us = keep.tile([P, PACK], F32, name="neg_us")
-        ident = keep.tile([P, P], F32, name="ident")
 
         for plane in (wn_plane, xt_plane, wt_plane):
             nc.vector.memset(plane[:].bitcast(I32), 0)
@@ -73,7 +71,6 @@ def tile_moe_expert_taught_by_page_kernel(
         for c in range(4):
             nc.sync.dma_start(run_tiles[c][:], run[c * P : (c + 1) * P, :])
 
-        make_identity(nc, ident[:])
         nc.vector.memset(d_codes[:, HALF:J], 0)
         nc.vector.memset(d_plane[:, HALF:J].bitcast(I32), 0)
         for window in windows:
@@ -104,7 +101,7 @@ def tile_moe_expert_taught_by_page_kernel(
         p_tiles = {}
         for h in range(2):
             for r in range(PACK):
-                acc = psum.tile([P, HALF], F32, name="p_acc", tag="mx", bufs=4)
+                acc = psum.tile([P, HALF], F32, name="p_acc", tag="mx", bufs=8)
                 nc.tensor.matmul_mx(
                     acc[:],
                     lhsT=wn_perm[:, 2 * P * r : 2 * P * (r + 1)].bitcast(E2M1X4),
@@ -135,7 +132,7 @@ def tile_moe_expert_taught_by_page_kernel(
             nc.vector.quantize_mx(d_codes[:, cols].bitcast(E5M2X4), d_plane[:, cols], d_half[:])
 
         def way_back(c):
-            acc = psum.tile([P, J], F32, name="q_acc", tag="mx", bufs=4)
+            acc = psum.tile([P, J], F32, name="q_acc", tag="mx", bufs=8)
             nc.tensor.matmul_mx(
                 acc[:],
                 lhsT=wt_tile[:, P * c : P * (c + 1)].bitcast(E4M3X4),
@@ -152,25 +149,10 @@ def tile_moe_expert_taught_by_page_kernel(
             nc.scalar.copy(q_part[:], acc[:, lo:hi])
             nc.vector.tensor_copy(window[:].indirect(offsets[:, lo // LANES : hi // LANES]), q_part[:])
 
-        def add_on_tensor_engine(c, window):
-            turned = keep.tile([P, T], F32, name="turned", tag="turned", bufs=2)
-            result = keep.tile([P, T], F32, name="result", tag="result", bufs=3)
-            for b in range(T // BANK):
-                bank = psum.tile([P, BANK], F32, name="sum_bank", tag="sum_bank", bufs=2)
-                for s in range(BANK // P):
-                    cols = slice(b * BANK + s * P, b * BANK + (s + 1) * P)
-                    here = slice(s * P, (s + 1) * P)
-                    nc.tensor.matmul(bank[:, here], run_tiles[c][:, cols], ident[:], start=True, stop=False, is_transpose=True)
-                    nc.tensor.matmul(bank[:, here], window[:, cols], ident[:], start=False, stop=True, is_transpose=True)
-                nc.scalar.copy(turned[:, b * BANK : (b + 1) * BANK], bank[:])
-            for b in range(T // BANK):
-                bank = psum.tile([P, BANK], F32, name="back_bank", tag="back_bank", bufs=2)
-                for s in range(BANK // P):
-                    cols = slice(b * BANK + s * P, b * BANK + (s + 1) * P)
-                    nc.tensor.transpose(bank[:, s * P : (s + 1) * P], turned[:, cols], ident[:])
-                cols = slice(b * BANK, (b + 1) * BANK)
-                nc.scalar.copy(result[:, cols], bank[:])
-                nc.scalar.dma_start(out[c * P : (c + 1) * P, cols], result[:, cols])
+        def add_on_gpsimd(c, window):
+            result = keep.tile([P, T], F32, name="result%d" % c)
+            nc.gpsimd.tensor_tensor(result[:], window[:], run_tiles[c][:], ADD)
+            nc.scalar.dma_start(out[c * P : (c + 1) * P, :], result[:])
 
         pairs0 = keep.tile([P, 2, HALF, 2], BF16, name="pairs0", align_bytes=64)
         pairs1 = keep.tile([P, 2, HALF, 2], BF16, name="pairs1", tag="after_weave1", align_bytes=64)
@@ -191,10 +173,10 @@ def tile_moe_expert_taught_by_page_kernel(
         scatter(late[0], windows[0], HALF, J, "late0")
         scatter(late[1], windows[1], HALF, J, "late1")
         scatter(late[2], windows[2], 0, J, "late2")
-        add_on_tensor_engine(0, windows[0])
+        add_on_gpsimd(0, windows[0])
         scatter(late[3], windows[0], 0, J, "late3")
-        add_on_tensor_engine(1, windows[1])
-        add_on_tensor_engine(2, windows[2])
+        add_on_gpsimd(1, windows[1])
+        add_on_gpsimd(2, windows[2])
         last = keep.tile([P, T], F32, name="last")
         for b in range(T // BANK):
             cols = slice(b * BANK, (b + 1) * BANK)

from contextlib import ExitStack

import concourse.mybir as mybir

K, N, T, J = 512, 512, 1024, 512
FLOPS = 2 * K * N * J * 2

F32 = mybir.dt.float32
BF16 = mybir.dt.bfloat16
I32 = mybir.dt.int32
U32 = mybir.dt.uint32
U16 = mybir.dt.uint16
U8 = mybir.dt.uint8
E4M3X4 = mybir.dt.float8_e4m3fn_x4
E5M2X4 = mybir.dt.float8_e5m2_x4
E2M1X4 = mybir.dt.float4_e2m1fn_x4
COPY = mybir.ActivationFunctionType.Copy
SUB = mybir.AluOpType.subtract
ADD = mybir.AluOpType.add

P = 128
PACK = 4
HALF = J // 2
LANES = 16
BANK = 512


def load_scale_rows(queue, plane, scales):
    for i in range(4):
        queue.dma_start(plane[i:P:32, :].bitcast(I32), scales[0, i:16:4, :].bitcast(I32))


def tile_moe_expert_taught_by_page_kernel(
    tc, xt_words, xt_scales, wn_words, wn_scales, te, us, wt_words, wt_scales, run, offs, out
):
    nc = tc.nc
    with ExitStack() as ctx:
        keep = ctx.enter_context(tc.tile_pool(name="keep", bufs=1))
        psum = ctx.enter_context(tc.psum_pool(name="psum", bufs=1))

        offsets = keep.tile([P, J // LANES], U16, name="offsets")
        wn_plane = keep.tile([P, N], U8, name="wn_plane", align_bytes=64)
        xt_plane = keep.tile([P, T], U8, name="xt_plane", align_bytes=64)
        wt_plane = keep.tile([P, K], U8, name="wt_plane", align_bytes=64)
        d_codes = keep.tile([P, J], I32, name="d_codes", align_bytes=64)
        d_plane = keep.tile([P, J], U8, name="d_plane", align_bytes=64)
        xt_tile = keep.tile([P, T], I32, name="xt_tile", align_bytes=64)
        wn_tile = keep.tile([P, 2 * N], U8, name="wn_tile", align_bytes=64)
        wt_tile = keep.tile([P, K], I32, name="wt_tile", align_bytes=64)
        te_tiles = [keep.tile([P, T], F32, name="te%d" % r) for r in range(PACK)]
        run_tiles = [keep.tile([P, T], F32, name="run%d" % c) for c in range(4)]
        windows = [keep.tile([P, T], F32, name="window%d" % w) for w in range(3)]
        us_tile = keep.tile([P, PACK], F32, name="us_tile")
        neg_us = keep.tile([P, PACK], F32, name="neg_us")

        for plane in (wn_plane, xt_plane, wt_plane):
            nc.vector.memset(plane[:].bitcast(I32), 0)

        nc.sync.dma_start(offsets[:], offs)
        load_scale_rows(nc.sync, wn_plane, wn_scales)
        nc.sync.dma_start(xt_tile[:], xt_words[0].rearrange("p t r -> p (t r)").bitcast(I32))
        nc.sync.dma_start(wn_tile[:].bitcast(I32), wn_words[0].bitcast(I32))
        te_rows = te.rearrange("(p r) t -> p r t", r=PACK)
        nc.sync.dma_start(te_tiles[0][:], te_rows[:, 0, :])
        load_scale_rows(nc.sync, xt_plane, xt_scales)
        for r in range(1, PACK):
            nc.sync.dma_start(te_tiles[r][:], te_rows[:, r, :])
        nc.gpsimd.dma_start(us_tile[:], us.rearrange("(p r) o -> p (r o)", r=PACK))
        nc.sync.dma_start(wt_tile[:], wt_words[0].rearrange("p k r -> p (k r)").bitcast(I32))
        load_scale_rows(nc.sync, wt_plane, wt_scales)
        for c in range(4):
            nc.sync.dma_start(run_tiles[c][:], run[c * P : (c + 1) * P, :])

        nc.vector.memset(d_codes[:, HALF:J], 0)
        nc.vector.memset(d_plane[:, HALF:J].bitcast(I32), 0)
        for window in windows:
            nc.vector.memset(window[:], 0.0)
        nc.scalar.mul(neg_us[:], us_tile[:], -1.0)

        wn_perm = keep.tile([P, 2 * N], U8, name="wn_perm", align_bytes=64)
        wn_plane_perm = keep.tile([P, N], U8, name="wn_plane_perm", align_bytes=64)
        nc.vector.tensor_copy(
            wn_plane_perm[:].rearrange("p (r m) -> p r m", r=PACK),
            wn_plane[:].rearrange("p (m r) -> p r m", r=PACK),
        )
        nc.vector.tensor_copy(
            wn_perm[:].bitcast(U16).rearrange("p (r m) -> p r m", r=PACK),
            wn_tile[:].bitcast(U16).rearrange("p (m r) -> p r m", r=PACK),
        )

        def listed(h):
            return offsets[:, h * HALF // LANES : (h + 1) * HALF // LANES]

        xg_words = [keep.tile([P, HALF], U32, name="xg_words%d" % h, align_bytes=64) for h in range(2)]
        xg_plane = [keep.tile([P, HALF], U8, name="xg_plane%d" % h, align_bytes=64) for h in range(2)]
        for h in range(2):
            nc.vector.tensor_copy(xg_words[h][:], xt_tile[:].bitcast(U32).indirect(listed(h)))
        for h in range(2):
            nc.vector.tensor_copy(xg_plane[h][:], xt_plane[:].indirect(listed(h)))

        p_tiles = {}
        for h in range(2):
            for r in range(PACK):
                acc = psum.tile([P, HALF], F32, name="p_acc", tag="mx", bufs=8)
                nc.tensor.matmul_mx(
                    acc[:],
                    lhsT=wn_perm[:, 2 * P * r : 2 * P * (r + 1)].bitcast(E2M1X4),
                    lhsT_scale=wn_plane_perm[:, P * r : P * (r + 1)],
                    rhs=xg_words[h][:].bitcast(E4M3X4),
                    rhs_scale=xg_plane[h][:],
                    start=True,
                    stop=True,
                )
                p_tiles[h, r] = keep.tile([P, HALF], F32, name="p%d_%d" % (h, r))
                nc.scalar.copy(p_tiles[h, r][:], acc[:])

        def difference(h, r, pairs, tag):
            diff = keep.tile([P, HALF], F32, name="diff%d_%d" % (h, r), tag=tag, align_bytes=64)
            nc.vector.tensor_tensor(diff[:], te_tiles[r][:].indirect(listed(h)), p_tiles[h, r][:], SUB)
            nc.scalar.activation(pairs[:, r // 2, :, r % 2], diff[:], COPY, scale=neg_us[:, r : r + 1])

        def weave(h, pairs, tag):
            d_half = keep.tile([P, HALF * PACK], BF16, name="d_half%d" % h, tag=tag, align_bytes=64)
            nc.scalar.copy(
                d_half[:].bitcast(F32).rearrange("p (j u) -> p j u", u=2),
                pairs[:].rearrange("p u j e -> p u (j e)").bitcast(F32).rearrange("p u j -> p j u"),
            )
            return d_half

        def quantise(h, d_half):
            cols = slice(h * HALF, (h + 1) * HALF)
            nc.vector.quantize_mx(d_codes[:, cols].bitcast(E5M2X4), d_plane[:, cols], d_half[:])

        def way_back(c):
            acc = psum.tile([P, J], F32, name="q_acc", tag="mx", bufs=8)
            nc.tensor.matmul_mx(
                acc[:],
                lhsT=wt_tile[:, P * c : P * (c + 1)].bitcast(E4M3X4),
                lhsT_scale=wt_plane[:, P * c : P * (c + 1)],
                rhs=d_codes[:].bitcast(E5M2X4),
                rhs_scale=d_plane[:],
                start=True,
                stop=True,
            )
            return acc

        def scatter(acc, window, lo, hi, tag):
            q_part = keep.tile([P, hi - lo], F32, name="q_" + tag, tag=tag, align_bytes=64)
            nc.scalar.copy(q_part[:], acc[:, lo:hi])
            nc.vector.tensor_copy(window[:].indirect(offsets[:, lo // LANES : hi // LANES]), q_part[:])

        def add_on_gpsimd(c, window):
            result = keep.tile([P, T], F32, name="result%d" % c)
            nc.gpsimd.tensor_tensor(result[:], window[:], run_tiles[c][:], ADD)
            nc.scalar.dma_start(out[c * P : (c + 1) * P, :], result[:])

        pairs0 = keep.tile([P, 2, HALF, 2], BF16, name="pairs0", align_bytes=64)
        pairs1 = keep.tile([P, 2, HALF, 2], BF16, name="pairs1", tag="after_weave1", align_bytes=64)
        for r in range(PACK):
            difference(0, r, pairs0, "diff0_%d" % r)
        d_first = weave(0, pairs0, "after_quantise0")
        difference(1, 0, pairs1, "diff1_0")
        difference(1, 1, pairs1, "diff1_1")
        quantise(0, d_first)
        early = [way_back(c) for c in range(2)]
        difference(1, 2, pairs1, "after_quantise0")
        difference(1, 3, pairs1, "diff1_3")
        scatter(early[0], windows[0], 0, HALF, "early0")
        d_second = weave(1, pairs1, "d_second")
        quantise(1, d_second)
        scatter(early[1], windows[1], 0, HALF, "after_weave1")
        late = [way_back(c) for c in range(4)]
        scatter(late[0], windows[0], HALF, J, "late0")
        scatter(late[1], windows[1], HALF, J, "late1")
        scatter(late[2], windows[2], 0, J, "late2")
        add_on_gpsimd(0, windows[0])
        scatter(late[3], windows[0], 0, J, "late3")
        add_on_gpsimd(1, windows[1])
        add_on_gpsimd(2, windows[2])
        last = keep.tile([P, T], F32, name="last")
        for b in range(T // BANK):
            cols = slice(b * BANK, (b + 1) * BANK)
            nc.vector.tensor_tensor(last[:, cols], windows[0][:, cols], run_tiles[3][:, cols], ADD)
            nc.sync.dma_start(out[3 * P : 4 * P, cols], last[:, cols])
